import numpy as np
import ml_dtypes


def mxq(x, axis, fmt="e4m3"):
    dtype, down = {"e4m3": (ml_dtypes.float8_e4m3fn, 7), "e5m2": (ml_dtypes.float8_e5m2, 14)}[fmt]
    v = np.moveaxis(np.asarray(x, np.float32).astype(ml_dtypes.bfloat16).astype(np.float64), axis, -1)
    blocks = v.reshape(v.shape[:-1] + (-1, 32))
    amax = np.abs(blocks).max(-1, keepdims=True)
    byte = np.maximum(np.where(amax > 0, np.frexp(amax)[1] - 1 + 127, 0) - down, 1)
    scale = np.exp2(byte - 127.0)
    codes = (blocks / scale).astype(np.float32).astype(dtype).astype(np.float64)
    return np.moveaxis((codes * scale).reshape(v.shape), -1, axis)


WIDE = False


def mx_kscale(k):
    if not WIDE:
        return np.ones(k)
    levels = np.array([10, -10, 5, -5, 0])
    if k % 512:
        return np.exp2(np.random.permutation(np.resize(levels, k // 32))).repeat(32)
    a = np.empty((k // 512, 16))
    for p in range(k // 512):
        a[p, :8] = np.random.permutation(np.resize(levels, 8))
        for g in range(8):
            far = levels[np.abs(levels - a[p, g]) >= 10]
            a[p, g + 8] = far[np.random.randint(len(far))]
    return np.exp2(a.ravel()).repeat(32)


def f64(x):
    return np.asarray(x).astype(np.float64)


def striped(idx):
    return np.tile(np.asarray(idx).reshape(-1, 16).T, (8, 1)).astype(np.uint16)


def unstriped(offs):
    return offs[:16].T.reshape(-1).astype(np.int64)


E2M1 = np.array([0.0, 0.5, 1.0, 1.5, 2.0, 3.0, 4.0, 6.0, -0.0, -0.5, -1.0, -1.5, -2.0, -3.0, -4.0, -6.0])


def pack_weight(w, fmt):
    k, n = w.shape
    w = f64(np.asarray(w, np.float32).astype(ml_dtypes.bfloat16)).reshape(k // 32, 32, n)
    amax = np.abs(w).max(1)
    if fmt == "e4m3":
        byte = np.frexp(amax)[1] - 1 + 127 - 7
    else:
        mant, ex = np.frexp(amax / 6.0)
        byte = np.where(mant > 0.5, ex, ex - 1) + 127
    byte = np.clip(np.where(amax > 0, byte, 1), 1, 254)
    scaled = (w * np.exp2(127.0 - byte)[:, None, :]).reshape(k, n).astype(np.float32)
    by_word = np.ascontiguousarray(scaled.reshape(k // 512, 128, 4, n).transpose(0, 1, 3, 2))
    if fmt == "e4m3":
        words = by_word.astype(ml_dtypes.float8_e4m3fn).view(np.uint8)
    else:
        c = by_word.astype(ml_dtypes.float4_e2m1fn).view(np.uint8) & 0xF
        words = (c[..., 0::2] | (c[..., 1::2] << 4)).reshape(k // 512, 128, 2 * n)
    return np.ascontiguousarray(words), np.ascontiguousarray(byte.astype(np.uint8).reshape(k // 512, 16, n))


def unpack_weight(words, scales, fmt):
    g, _, n = scales.shape
    words = np.ascontiguousarray(words).reshape(g, 128, n, -1)
    if fmt == "e4m3":
        vals = words.view(ml_dtypes.float8_e4m3fn).astype(np.float64)
    else:
        nib = np.empty((g, 128, n, 4), np.uint8)
        nib[..., 0::2] = words & 0xF
        nib[..., 1::2] = words >> 4
        vals = E2M1[nib]
    vals = vals * np.repeat(np.exp2(scales.astype(np.float64) - 127.0), 8, axis=1)[..., None]
    return vals.transpose(0, 1, 3, 2).reshape(g * 512, n)


def sigmoid(v):
    return 1.0 / (1.0 + np.exp(-v))


D, E, T, I, Q, G = 512, 512, 2048, 512, 128, 32


def setup_inputs():
    n = np.random.standard_normal
    idx = np.random.permutation(T)[:I]
    fd = mx_kscale(D)
    fi = mx_kscale(I)
    ti = np.ones(T)
    ti[idx] = fi
    keysp = pack_weight(n((D, T)) / fd[:, None], "e2m1")
    return {
        "query": (n((D, Q)) * 0.8 / np.sqrt(D) * fd[:, None]).astype(np.float32),
        "keys_words": keysp[0],
        "keys_scales": keysp[1],
        "th": (np.random.uniform(-0.5, 0.5, (Q, 1))).astype(np.float32),
        "sharp": (np.random.uniform(1.0, 3.0, (Q, 1))).astype(np.float32),
        "dquery": (n((D, Q)) * 0.6 / np.sqrt(D) * fd[:, None]).astype(np.float32),
        "os": (np.random.uniform(0.5, 2.0, (1, I)) * fi).astype(np.float32),
        "vals": (n((E, T)) / ti).astype(np.float32),
        "offs": striped(idx),
    }


def reference(query, keys_words, keys_scales, th, sharp, dquery, os, vals, offs):
    idx = unstriped(offs)
    keysu = unpack_weight(keys_words, keys_scales, "e2m1")
    queryq = mxq(f64(query), 0, "e4m3")
    keysidxg = keysu[:, idx]
    a = queryq.T @ keysidxg
    dqueryq = mxq(f64(dquery), 0, "e4m3")
    ta = dqueryq.T @ keysidxg
    s = a.reshape(Q, G, I // G).mean(axis=2) * f64(sharp)
    p = np.exp(s - np.max(s, axis=1, keepdims=True))
    z = np.sum(p, axis=1, keepdims=True)
    r = p / z
    rr = np.repeat(r, I // G, axis=1)
    ts = ta.reshape(Q, G, I // G).mean(axis=2) * f64(sharp)
    tp = ts * p
    tz = np.sum(tp, axis=1, keepdims=True)
    tr = (tp - tz * p / z) / z
    trr = np.repeat(tr, I // G, axis=1)
    tw = trr * sigmoid(a - f64(th)) + ta * sigmoid(a - f64(th)) * (1.0 - sigmoid(a - f64(th))) * rr
    wo1 = tw * f64(os)
    wt1 = wo1.T
    vt1 = f64(vals)[:, idx].T
    wt1q = mxq(wt1, 0, "e4m3")
    vt1q = mxq(vt1, 0, "e4m3")
    o = wt1q.T @ vt1q
    return o

@@ -1,0 +1,211 @@
+from contextlib import ExitStack
+
+import concourse.mybir as mybir
+from concourse.masks import make_identity
+
+D, E, T, I, Q, G = 512, 512, 2048, 512, 128, 32
+FLOPS = 2 * (2 * Q * D * I + Q * I * E)
+
+F32 = mybir.dt.float32
+BF16 = mybir.dt.bfloat16
+I32 = mybir.dt.int32
+U32 = mybir.dt.uint32
+U16 = mybir.dt.uint16
+U8 = mybir.dt.uint8
+FP8X4 = mybir.dt.float8_e4m3fn_x4
+FP4X4 = mybir.dt.float4_e2m1fn_x4
+ALU = mybir.AluOpType
+ACT = mybir.ActivationFunctionType
+AX = mybir.AxisListType
+
+P = 128
+PACK = 4
+PAGE = I // G
+PARTS_PER_PAGE = PAGE // PACK
+PLANES = E // P
+
+
+def tile_attend_ttpagetimessigmoid_kernel(tc, query, keys_words, keys_scales, th, sharp, dquery, slot_factor, vals, offs, out):
+    nc = tc.nc
+    with ExitStack() as ctx:
+        sb = ctx.enter_context(tc.tile_pool(name="sb", bufs=1))
+        ps = ctx.enter_context(tc.psum_pool(name="ps", bufs=1))
+
+        offsets = sb.tile([P, I // 16], U16, name="offsets")
+        nc.sync.dma_start(offsets[:], offs)
+        words = sb.tile([P, T], U16, name="words", align_bytes=64)
+        nc.sync.dma_start(words[:].bitcast(I32), keys_words[0].bitcast(I32))
+        kscales = sb.tile([P, T], U8, name="kscales", align_bytes=64)
+        nc.vector.memset(kscales[:].bitcast(I32), 0)
+        for quad in range(4):
+            nc.scalar.dma_start(
+                kscales[32 * quad : 32 * quad + 4, :].bitcast(I32),
+                keys_scales[0, 4 * quad : 4 * quad + 4, :].bitcast(I32),
+            )
+        q_raw = [sb.tile([P, PACK, Q], F32, name=f"q_raw{k}") for k in range(2)]
+        for k, src in enumerate((query, dquery)):
+            nc.sync.dma_start(q_raw[k][:], src.rearrange("(p t) q -> p t q", t=PACK))
+        pool_vals = [sb.tile([P, T], F32, name=f"pool_vals{c}", align_bytes=64) for c in range(PLANES)]
+        th_sb = sb.tile([P, 1], F32, name="th_sb")
+        sharp_sb = sb.tile([P, 1], F32, name="sharp_sb")
+        os_sb = sb.tile([P, PACK], F32, name="os_sb")
+        nc.sync.dma_start(pool_vals[0][:], vals[0:P, :])
+        nc.sync.dma_start(th_sb[:], th)
+        nc.sync.dma_start(sharp_sb[:], sharp)
+        nc.sync.dma_start(os_sb[:], slot_factor.rearrange("o (p t) -> (o p) t", t=PACK))
+        for c in range(1, PLANES):
+            nc.sync.dma_start(pool_vals[c][:], vals[c * P : (c + 1) * P, :])
+
+        ident = sb.tile([P, P], F32, name="ident")
+        make_identity(nc, ident[:])
+        warm_out = sb.tile([P, 1], F32, name="warm_out")
+        warm_in = sb.tile([P, 1], F32, name="warm_in")
+        nc.gpsimd.memset(warm_in[:], 0.0)
+        nc.scalar.activation(warm_out[:], warm_in[:], ACT.Sigmoid)
+        neg_th = sb.tile([P, 1], F32, name="neg_th")
+        nc.scalar.activation(neg_th[:], th_sb[:], ACT.Copy, scale=-1.0)
+        neg_sharp = sb.tile([P, 1], F32, name="neg_sharp")
+        nc.scalar.activation(neg_sharp[:], sharp_sb[:], ACT.Copy, scale=-1.0 / PAGE)
+
+        key_words = sb.tile([P, I], U16, name="key_words", align_bytes=64)
+        nc.vector.tensor_copy(key_words[:], words[:].indirect(offsets[:]))
+        key_scales = sb.tile([P, I], U8, name="key_scales", align_bytes=64)
+        nc.vector.tensor_copy(key_scales[:], kscales[:].indirect(offsets[:]))
+
+        q_bf = sb.tile([P, 2, Q, PACK], BF16, name="q_bf", align_bytes=64)
+        for k in range(2):
+            nc.scalar.copy(
+                q_bf[:, k].rearrange("p (c i) t -> p c t i", i=4),
+                q_raw[k][:].rearrange("p t (c i) -> p c t i", i=4),
+            )
+        q_codes = sb.tile([P, 2 * Q], U32, name="q_codes", align_bytes=64)
+        q_scales = sb.tile([P, 2 * Q], U8, name="q_scales", align_bytes=64)
+        nc.vector.quantize_mx(
+            out=q_codes[:].bitcast(FP8X4), scales=q_scales[:], in_=q_bf[:].rearrange("p k q t -> p (k q t)")
+        )
+        a_ps = ps.tile([P, I], F32, name="a_ps")
+        ta_ps = ps.tile([P, I], F32, name="ta_ps")
+        for k, bank in enumerate((a_ps, ta_ps)):
+            nc.tensor.matmul_mx(
+                out=bank[:],
+                lhsT=q_codes[:, k * Q : (k + 1) * Q].bitcast(FP8X4),
+                lhsT_scale=q_scales[:, k * Q : (k + 1) * Q],
+                rhs=key_words[:].bitcast(FP4X4),
+                rhs_scale=key_scales[:],
+                start=True,
+                stop=True,
+            )
+
+        v_codes = [sb.tile([P, P], U32, name=f"v_codes{c}", align_bytes=64) for c in range(PLANES)]
+        v_scales = [sb.tile([P, P], U8, name=f"v_scales{c}", align_bytes=64) for c in range(PLANES)]
+
+        def values_plane(c):
+            picked = sb.tile([P, I], BF16, name=f"picked{c}", align_bytes=64)
+            nc.vector.tensor_copy(picked[:], pool_vals[c][:].indirect(offsets[:]))
+            pairs = picked[:].bitcast(F32)
+            turned = ps.tile([P, 2, P], F32, name="turned", tag="turned", bufs=2)
+            for u in range(2):
+                nc.tensor.transpose(turned[:, u, :], pairs[:, u : I // 2 : 2], ident[:])
+            v_bf = sb.tile([P, P * PACK], BF16, name=f"v_bf{c}", align_bytes=64)
+            nc.scalar.copy(
+                v_bf[:].bitcast(F32).rearrange("p (e u) -> p e u", u=2), turned[:].rearrange("p u e -> p e u")
+            )
+            return v_bf
+
+        def quantise_plane(c, v_bf):
+            nc.vector.quantize_mx(out=v_codes[c][:].bitcast(FP8X4), scales=v_scales[c][:], in_=v_bf[:])
+
+        v0 = values_plane(0)
+
+        dealt = "q (p t) -> q t p"
+        gate = sb.tile([P, PACK, P], F32, name="gate")
+        nc.scalar.activation(gate[:], a_ps[:].rearrange(dealt, t=PACK), ACT.Sigmoid, bias=neg_th[:])
+        ungate = sb.tile([P, PACK, P], F32, name="ungate")
+        nc.scalar.activation(ungate[:], a_ps[:].rearrange(dealt, t=PACK), ACT.Sigmoid, bias=th_sb[:], scale=-1.0)
+
+        a_sum = sb.tile([P, G], F32, name="a_sum")
+        nc.vector.tensor_reduce(a_sum[:], a_ps[:].rearrange("q (g j) -> q g j", j=PAGE), AX.X, ALU.add)
+        neg_s = sb.tile([P, G], F32, name="neg_s")
+        neg_max = sb.tile([P, 1], F32, name="neg_max")
+        nc.vector.tensor_scalar(neg_s[:], a_sum[:], neg_sharp[:], None, ALU.mult, ALU.min, accum_out=neg_max[:])
+        ta_sum = sb.tile([P, G], F32, name="ta_sum")
+        nc.vector.tensor_reduce(ta_sum[:], ta_ps[:].rearrange("q (g j) -> q g j", j=PAGE), AX.X, ALU.add)
+        num = sb.tile([P, G], F32, name="num")
+        nc.scalar.activation(num[:], neg_s[:], ACT.Sigmoid, bias=neg_max[:], scale=-1.0)
+        den = sb.tile([P, G], F32, name="den")
+        nc.scalar.activation(den[:], num[:], ACT.Copy, bias=1.0, scale=-1.0)
+        x = sb.tile([P, PACK, P], F32, name="x")
+        nc.vector.tensor_tensor(x[:], ta_ps[:].rearrange(dealt, t=PACK), ungate[:], ALU.mult)
+
+        gate_t = ps.tile([P, PACK, Q], F32, name="gate_t")
+        for t in range(PACK):
+            nc.tensor.transpose(gate_t[:, t, :], gate[:, t, :], ident[:])
+        gate_os = sb.tile([P, PACK, Q], F32, name="gate_os")
+        for t in range(PACK):
+            nc.scalar.activation(gate_os[:, t, :], gate_t[:, t, :], ACT.Copy, scale=os_sb[:, t : t + 1])
+
+        quantise_plane(0, v0)
+        inv_den = sb.tile([P, G], F32, name="inv_den")
+        nc.vector.reciprocal(inv_den[:], den[:])
+        pexp = sb.tile([P, G], F32, name="pexp")
+        z = sb.tile([P, 1], F32, name="z")
+        nc.vector.scalar_tensor_tensor(pexp[:], num[:], 1.0, inv_den[:], ALU.mult, ALU.mult, accum_out=z[:])
+        inv_z = sb.tile([P, 1], F32, name="inv_z")
+        nc.vector.reciprocal(inv_z[:], z[:])
+        by_part = [P, G, PARTS_PER_PAGE]
+        share = sb.tile(by_part, F32, name="share")
+        nc.vector.tensor_scalar(share[:], pexp[:].unsqueeze(2).to_broadcast(by_part), inv_z[:], None, ALU.mult)
+        neg_tsr = sb.tile([P, G], F32, name="neg_tsr")
+        neg_mean = sb.tile([P, 1], F32, name="neg_mean")
+        nc.vector.scalar_tensor_tensor(
+            neg_tsr[:], ta_sum[:], neg_sharp[:], share[:, :, 0], ALU.mult, ALU.mult, accum_out=neg_mean[:]
+        )
+        xr = sb.tile([P, PACK, P], F32, name="xr")
+        share_flat = share[:].rearrange("q g j -> q (g j)")
+        nc.vector.tensor_tensor(xr[:], x[:], share_flat.unsqueeze(1).to_broadcast([P, PACK, P]), ALU.mult)
+        tshare = sb.tile(by_part, F32, name="tshare")
+        nc.vector.scalar_tensor_tensor(
+            tshare[:], share[:], neg_mean[:], neg_tsr[:].unsqueeze(2).to_broadcast(by_part), ALU.mult, ALU.subtract
+        )
+        v1 = values_plane(1)
+        inner_t = ps.tile([P, PACK, Q], F32, name="inner_t")
+        for t in range(PACK):
+            nc.tensor.matmul(inner_t[:, t, :], xr[:, t, :], ident[:], start=True, stop=False, is_transpose=True)
+            nc.tensor.matmul(
+                inner_t[:, t, :], tshare[:].rearrange("q g j -> q (g j)"), ident[:],
+                start=False, stop=True, is_transpose=True,
+            )
+        v2 = values_plane(2)
+        quantise_plane(1, v1)
+        w_bf = sb.tile([P, Q, PACK], BF16, name="w_bf", align_bytes=64)
+        nc.vector.tensor_tensor(
+            w_bf[:].rearrange("p (c i) t -> p c t i", i=4),
+            inner_t[:].rearrange("p t (c i) -> p c t i", i=4),
+            gate_os[:].rearrange("p t (c i) -> p c t i", i=4),
+            ALU.mult,
+        )
+        quantise_plane(2, v2)
+        w_codes = sb.tile([P, Q], U32, name="w_codes", align_bytes=64)
+        w_scales = sb.tile([P, Q], U8, name="w_scales", align_bytes=64)
+        nc.vector.quantize_mx(
+            out=w_codes[:].bitcast(FP8X4), scales=w_scales[:], in_=w_bf[:].rearrange("p q t -> p (q t)")
+        )
+        v3 = values_plane(3)
+        quantise_plane(3, v3)
+
+        for name, planes in (("head", range(PLANES - 1)), ("tail", range(PLANES - 1, PLANES))):
+            width = len(planes) * P
+            o_ps = ps.tile([P, width], F32, name=f"o_ps_{name}")
+            for n, c in enumerate(planes):
+                nc.tensor.matmul_mx(
+                    out=o_ps[:, n * P : (n + 1) * P],
+                    lhsT=w_codes[:].bitcast(FP8X4),
+                    lhsT_scale=w_scales[:],
+                    rhs=v_codes[c][:].bitcast(FP8X4),
+                    rhs_scale=v_scales[c][:],
+                    start=True,
+                    stop=True,
+                )
+            o_sb = sb.tile([P, width], F32, name=f"o_sb_{name}")
+            nc.scalar.copy(o_sb[:], o_ps[:])
+            nc.sync.dma_start(out[:, planes[0] * P : planes[0] * P + width], o_sb[:])

@@ -38,30 +38,27 @@ def tile_attend_ttpagetimessigmoid_kernel(tc, query, keys_words, keys_scales, th
         kscales = sb.tile([P, T], U8, name="kscales", align_bytes=64)
         nc.vector.memset(kscales[:].bitcast(I32), 0)
         for quad in range(4):
-            nc.scalar.dma_start(
+            nc.sync.dma_start(
                 kscales[32 * quad : 32 * quad + 4, :].bitcast(I32),
                 keys_scales[0, 4 * quad : 4 * quad + 4, :].bitcast(I32),
             )
         q_raw = [sb.tile([P, PACK, Q], F32, name=f"q_raw{k}") for k in range(2)]
         for k, src in enumerate((query, dquery)):
             nc.sync.dma_start(q_raw[k][:], src.rearrange("(p t) q -> p t q", t=PACK))
-        pool_vals = [sb.tile([P, T], F32, name=f"pool_vals{c}", align_bytes=64) for c in range(PLANES)]
+        pool_vals = [sb.tile([P, T], F32, name=f"pool_vals{c}", tag=f"plane{c}", align_bytes=64) for c in range(PLANES)]
         th_sb = sb.tile([P, 1], F32, name="th_sb")
         sharp_sb = sb.tile([P, 1], F32, name="sharp_sb")
         os_sb = sb.tile([P, PACK], F32, name="os_sb")
         nc.sync.dma_start(pool_vals[0][:], vals[0:P, :])
-        nc.sync.dma_start(th_sb[:], th)
         nc.sync.dma_start(sharp_sb[:], sharp)
+        nc.sync.dma_start(th_sb[:], th)
+        nc.sync.dma_start(pool_vals[1][:], vals[P : 2 * P, :])
         nc.sync.dma_start(os_sb[:], slot_factor.rearrange("o (p t) -> (o p) t", t=PACK))
-        for c in range(1, PLANES):
+        for c in range(2, PLANES):
             nc.sync.dma_start(pool_vals[c][:], vals[c * P : (c + 1) * P, :])
 
         ident = sb.tile([P, P], F32, name="ident")
         make_identity(nc, ident[:])
-        warm_out = sb.tile([P, 1], F32, name="warm_out")
-        warm_in = sb.tile([P, 1], F32, name="warm_in")
-        nc.gpsimd.memset(warm_in[:], 0.0)
-        nc.scalar.activation(warm_out[:], warm_in[:], ACT.Sigmoid)
         neg_th = sb.tile([P, 1], F32, name="neg_th")
         nc.scalar.activation(neg_th[:], th_sb[:], ACT.Copy, scale=-1.0)
         neg_sharp = sb.tile([P, 1], F32, name="neg_sharp")
@@ -96,78 +93,80 @@ def tile_attend_ttpagetimessigmoid_kernel(tc, query, keys_words, keys_scales, th
                 stop=True,
             )
 
-        v_codes = [sb.tile([P, P], U32, name=f"v_codes{c}", align_bytes=64) for c in range(PLANES)]
-        v_scales = [sb.tile([P, P], U8, name=f"v_scales{c}", align_bytes=64) for c in range(PLANES)]
-
-        def values_plane(c):
-            picked = sb.tile([P, I], BF16, name=f"picked{c}", align_bytes=64)
+        def gather_plane(c):
+            picked = sb.tile([P, I], BF16, name=f"picked{c}", tag=f"picked{c}", align_bytes=64)
             nc.vector.tensor_copy(picked[:], pool_vals[c][:].indirect(offsets[:]))
             pairs = picked[:].bitcast(F32)
             turned = ps.tile([P, 2, P], F32, name="turned", tag="turned", bufs=2)
             for u in range(2):
                 nc.tensor.transpose(turned[:, u, :], pairs[:, u : I // 2 : 2], ident[:])
-            v_bf = sb.tile([P, P * PACK], BF16, name=f"v_bf{c}", align_bytes=64)
+            return turned
+
+        def weave_plane(v_bf, turned):
             nc.scalar.copy(
-                v_bf[:].bitcast(F32).rearrange("p (e u) -> p e u", u=2), turned[:].rearrange("p u e -> p e u")
+                v_bf.bitcast(F32).rearrange("p (e u) -> p e u", u=2), turned[:].rearrange("p u e -> p e u")
             )
-            return v_bf
 
-        def quantise_plane(c, v_bf):
-            nc.vector.quantize_mx(out=v_codes[c][:].bitcast(FP8X4), scales=v_scales[c][:], in_=v_bf[:])
-
-        v0 = values_plane(0)
+        def quantise(name, values, tag=""):
+            width = values.shape[1] // PACK
+            codes = sb.tile([P, width], U32, name=f"{name}_codes", tag=tag, align_bytes=64)
+            scales = sb.tile([P, width], U8, name=f"{name}_scales", align_bytes=64)
+            nc.vector.quantize_mx(out=codes[:].bitcast(FP8X4), scales=scales[:], in_=values)
+            return codes, scales
 
         dealt = "q (p t) -> q t p"
-        gate = sb.tile([P, PACK, P], F32, name="gate")
-        nc.scalar.activation(gate[:], a_ps[:].rearrange(dealt, t=PACK), ACT.Sigmoid, bias=neg_th[:])
-        ungate = sb.tile([P, PACK, P], F32, name="ungate")
-        nc.scalar.activation(ungate[:], a_ps[:].rearrange(dealt, t=PACK), ACT.Sigmoid, bias=th_sb[:], scale=-1.0)
-
-        a_sum = sb.tile([P, G], F32, name="a_sum")
+        a_sum = sb.tile([P, G], F32, name="a_sum", tag="picked0", align_bytes=64)
+        ta_sum = sb.tile([P, G], F32, name="ta_sum")
         nc.vector.tensor_reduce(a_sum[:], a_ps[:].rearrange("q (g j) -> q g j", j=PAGE), AX.X, ALU.add)
         neg_s = sb.tile([P, G], F32, name="neg_s")
-        neg_max = sb.tile([P, 1], F32, name="neg_max")
+        neg_max = sb.tile([P, 1], F32, name="neg_max", tag="gate", align_bytes=64)
         nc.vector.tensor_scalar(neg_s[:], a_sum[:], neg_sharp[:], None, ALU.mult, ALU.min, accum_out=neg_max[:])
-        ta_sum = sb.tile([P, G], F32, name="ta_sum")
         nc.vector.tensor_reduce(ta_sum[:], ta_ps[:].rearrange("q (g j) -> q g j", j=PAGE), AX.X, ALU.add)
-        num = sb.tile([P, G], F32, name="num")
-        nc.scalar.activation(num[:], neg_s[:], ACT.Sigmoid, bias=neg_max[:], scale=-1.0)
-        den = sb.tile([P, G], F32, name="den")
-        nc.scalar.activation(den[:], num[:], ACT.Copy, bias=1.0, scale=-1.0)
-        x = sb.tile([P, PACK, P], F32, name="x")
-        nc.vector.tensor_tensor(x[:], ta_ps[:].rearrange(dealt, t=PACK), ungate[:], ALU.mult)
+        by_part = [P, G, PARTS_PER_PAGE]
+        pexp = sb.tile(by_part, F32, name="pexp")
+        z4 = sb.tile([P, 1], F32, name="z4")
+        nc.scalar.activation(
+            pexp[:], neg_s[:].unsqueeze(2).to_broadcast(by_part), ACT.Exp, bias=neg_max[:], scale=-1.0, accum_out=z4[:]
+        )
+        turned0 = gather_plane(0)
 
+        gate = sb.tile([P, PACK, P], F32, name="gate", tag="gate", align_bytes=64)
+        nc.scalar.activation(gate[:], a_ps[:].rearrange(dealt, t=PACK), ACT.Sigmoid, bias=neg_th[:])
+        v_bf0 = sb.tile([P, P * PACK], BF16, name="v_bf0", align_bytes=64)
+        weave_plane(v_bf0[:], turned0)
+        v_bf12 = sb.tile([P, 2, P * PACK], BF16, name="v_bf12", align_bytes=64)
+        weave_plane(v_bf12[:, 0, :], gather_plane(1))
+        neg_os4 = sb.tile([P, PACK], F32, name="neg_os4")
+        nc.scalar.activation(neg_os4[:], os_sb[:], ACT.Copy, scale=-1.0 * PARTS_PER_PAGE)
         gate_t = ps.tile([P, PACK, Q], F32, name="gate_t")
         for t in range(PACK):
             nc.tensor.transpose(gate_t[:, t, :], gate[:, t, :], ident[:])
-        gate_os = sb.tile([P, PACK, Q], F32, name="gate_os")
+        gate_os = sb.tile([P, PACK, Q], F32, name="gate_os", tag="gate_os", align_bytes=64)
         for t in range(PACK):
-            nc.scalar.activation(gate_os[:, t, :], gate_t[:, t, :], ACT.Copy, scale=os_sb[:, t : t + 1])
+            nc.scalar.activation(gate_os[:, t, :], gate_t[:, t, :], ACT.Copy, scale=neg_os4[:, t : t + 1])
 
-        quantise_plane(0, v0)
-        inv_den = sb.tile([P, G], F32, name="inv_den")
-        nc.vector.reciprocal(inv_den[:], den[:])
-        pexp = sb.tile([P, G], F32, name="pexp")
-        z = sb.tile([P, 1], F32, name="z")
-        nc.vector.scalar_tensor_tensor(pexp[:], num[:], 1.0, inv_den[:], ALU.mult, ALU.mult, accum_out=z[:])
-        inv_z = sb.tile([P, 1], F32, name="inv_z")
-        nc.vector.reciprocal(inv_z[:], z[:])
-        by_part = [P, G, PARTS_PER_PAGE]
-        share = sb.tile(by_part, F32, name="share")
-        nc.vector.tensor_scalar(share[:], pexp[:].unsqueeze(2).to_broadcast(by_part), inv_z[:], None, ALU.mult)
-        neg_tsr = sb.tile([P, G], F32, name="neg_tsr")
-        neg_mean = sb.tile([P, 1], F32, name="neg_mean")
+        inv_z4 = sb.tile([P, 1], F32, name="inv_z4")
+        nc.vector.reciprocal(inv_z4[:], z4[:])
+        neg_tp = sb.tile(by_part, F32, name="neg_tp")
+        neg_tz4 = sb.tile([P, 1], F32, name="neg_tz4")
         nc.vector.scalar_tensor_tensor(
-            neg_tsr[:], ta_sum[:], neg_sharp[:], share[:, :, 0], ALU.mult, ALU.mult, accum_out=neg_mean[:]
+            neg_tp[:], ta_sum[:].unsqueeze(2).to_broadcast(by_part), neg_sharp[:], pexp[:],
+            ALU.mult, ALU.mult, accum_out=neg_tz4[:],
         )
-        xr = sb.tile([P, PACK, P], F32, name="xr")
-        share_flat = share[:].rearrange("q g j -> q (g j)")
-        nc.vector.tensor_tensor(xr[:], x[:], share_flat.unsqueeze(1).to_broadcast([P, PACK, P]), ALU.mult)
+        inv_sq = sb.tile([P, 1], F32, name="inv_sq")
+        nc.vector.tensor_tensor(inv_sq[:], inv_z4[:], inv_z4[:], ALU.mult)
+        tar = sb.tile([P, PACK, P], F32, name="tar", tag="picked2", align_bytes=64)
+        nc.vector.scalar_tensor_tensor(
+            tar[:], ta_ps[:].rearrange(dealt, t=PACK), inv_z4[:],
+            pexp[:].rearrange("q g j -> q (g j)").unsqueeze(1).to_broadcast([P, PACK, P]), ALU.mult, ALU.mult,
+        )
+        mean_term = sb.tile(by_part, F32, name="mean_term")
+        nc.vector.tensor_scalar(mean_term[:], pexp[:], neg_tz4[:], inv_sq[:], ALU.mult, ALU.mult)
         tshare = sb.tile(by_part, F32, name="tshare")
-        nc.vector.scalar_tensor_tensor(
-            tshare[:], share[:], neg_mean[:], neg_tsr[:].unsqueeze(2).to_broadcast(by_part), ALU.mult, ALU.subtract
-        )
-        v1 = values_plane(1)
+        nc.vector.scalar_tensor_tensor(tshare[:], neg_tp[:], inv_z4[:], mean_term[:], ALU.mult, ALU.subtract)
+        xr = sb.tile([P, PACK, P], F32, name="xr", tag="plane1", align_bytes=64)
+        nc.vector.scalar_tensor_tensor(xr[:], gate[:], 1.0, tar[:], ALU.subtract, ALU.mult)
+        v0_codes, v0_scales = quantise("v0", v_bf0[:])
         inner_t = ps.tile([P, PACK, Q], F32, name="inner_t")
         for t in range(PACK):
             nc.tensor.matmul(inner_t[:, t, :], xr[:, t, :], ident[:], start=True, stop=False, is_transpose=True)
@@ -175,37 +174,39 @@ def tile_attend_ttpagetimessigmoid_kernel(tc, query, keys_words, keys_scales, th
                 inner_t[:, t, :], tshare[:].rearrange("q g j -> q (g j)"), ident[:],
                 start=False, stop=True, is_transpose=True,
             )
-        v2 = values_plane(2)
-        quantise_plane(1, v1)
-        w_bf = sb.tile([P, Q, PACK], BF16, name="w_bf", align_bytes=64)
+        weave_plane(v_bf12[:, 1, :], gather_plane(2))
+        v_bf3 = sb.tile([P, P * PACK], BF16, name="v_bf3", align_bytes=64)
+        weave_plane(v_bf3[:], gather_plane(3))
+        w_bf = sb.tile([P, Q, PACK], BF16, name="w_bf", tag="plane3", align_bytes=64)
         nc.vector.tensor_tensor(
             w_bf[:].rearrange("p (c i) t -> p c t i", i=4),
             inner_t[:].rearrange("p t (c i) -> p c t i", i=4),
             gate_os[:].rearrange("p t (c i) -> p c t i", i=4),
             ALU.mult,
         )
-        quantise_plane(2, v2)
-        w_codes = sb.tile([P, Q], U32, name="w_codes", align_bytes=64)
-        w_scales = sb.tile([P, Q], U8, name="w_scales", align_bytes=64)
-        nc.vector.quantize_mx(
-            out=w_codes[:].bitcast(FP8X4), scales=w_scales[:], in_=w_bf[:].rearrange("p q t -> p (q t)")
-        )
-        v3 = values_plane(3)
-        quantise_plane(3, v3)
+        w_codes, w_scales = quantise("w", w_bf[:].rearrange("p q t -> p (q t)"))
+        v12_codes, v12_scales = quantise("v12", v_bf12[:].rearrange("p c x -> p (c x)"), tag="gate_os")
+        v3_codes, v3_scales = quantise("v3", v_bf3[:])
 
-        for name, planes in (("head", range(PLANES - 1)), ("tail", range(PLANES - 1, PLANES))):
-            width = len(planes) * P
-            o_ps = ps.tile([P, width], F32, name=f"o_ps_{name}")
-            for n, c in enumerate(planes):
-                nc.tensor.matmul_mx(
-                    out=o_ps[:, n * P : (n + 1) * P],
-                    lhsT=w_codes[:].bitcast(FP8X4),
-                    lhsT_scale=w_scales[:],
-                    rhs=v_codes[c][:].bitcast(FP8X4),
-                    rhs_scale=v_scales[c][:],
-                    start=True,
-                    stop=True,
-                )
-            o_sb = sb.tile([P, width], F32, name=f"o_sb_{name}")
-            nc.scalar.copy(o_sb[:], o_ps[:])
-            nc.sync.dma_start(out[:, planes[0] * P : planes[0] * P + width], o_sb[:])
+        def weigh(bank, codes, scales):
+            nc.tensor.matmul_mx(
+                out=bank,
+                lhsT=w_codes[:].bitcast(FP8X4),
+                lhsT_scale=w_scales[:],
+                rhs=codes[:].bitcast(FP8X4),
+                rhs_scale=scales[:],
+                start=True,
+                stop=True,
+            )
+
+        head_ps = ps.tile([P, 3 * P], F32, name="head_ps")
+        weigh(head_ps[:, 0:P], v0_codes, v0_scales)
+        weigh(head_ps[:, P : 3 * P], v12_codes, v12_scales)
+        tail_ps = ps.tile([P, P], F32, name="tail_ps")
+        weigh(tail_ps[:], v3_codes, v3_scales)
+        head_sb = sb.tile([P, 3 * P], F32, name="head_sb")
+        nc.scalar.copy(head_sb[:], head_ps[:])
+        nc.sync.dma_start(out[:, 0 : 3 * P], head_sb[:])
+        tail_sb = sb.tile([P, P], F32, name="tail_sb")
+        nc.vector.tensor_copy(tail_sb[:], tail_ps[:])
+        nc.sync.dma_start(out[:, 3 * P : E], tail_sb[:])

from contextlib import ExitStack

import concourse.mybir as mybir
from concourse.masks import make_identity

D, E, T, I, Q, G = 512, 512, 2048, 512, 128, 32
FLOPS = 2 * (2 * Q * D * I + Q * I * E)

F32 = mybir.dt.float32
BF16 = mybir.dt.bfloat16
I32 = mybir.dt.int32
U32 = mybir.dt.uint32
U16 = mybir.dt.uint16
U8 = mybir.dt.uint8
FP8X4 = mybir.dt.float8_e4m3fn_x4
FP4X4 = mybir.dt.float4_e2m1fn_x4
ALU = mybir.AluOpType
ACT = mybir.ActivationFunctionType
AX = mybir.AxisListType

P = 128
PACK = 4
PAGE = I // G
PARTS_PER_PAGE = PAGE // PACK
PLANES = E // P


def tile_attend_ttpagetimessigmoid_kernel(tc, query, keys_words, keys_scales, th, sharp, dquery, slot_factor, vals, offs, out):
    nc = tc.nc
    with ExitStack() as ctx:
        sb = ctx.enter_context(tc.tile_pool(name="sb", bufs=1))
        ps = ctx.enter_context(tc.psum_pool(name="ps", bufs=1))

        offsets = sb.tile([P, I // 16], U16, name="offsets")
        nc.sync.dma_start(offsets[:], offs)
        words = sb.tile([P, T], U16, name="words", align_bytes=64)
        nc.sync.dma_start(words[:].bitcast(I32), keys_words[0].bitcast(I32))
        kscales = sb.tile([P, T], U8, name="kscales", align_bytes=64)
        nc.vector.memset(kscales[:].bitcast(I32), 0)
        for quad in range(4):
            nc.sync.dma_start(
                kscales[32 * quad : 32 * quad + 4, :].bitcast(I32),
                keys_scales[0, 4 * quad : 4 * quad + 4, :].bitcast(I32),
            )
        q_raw = [sb.tile([P, PACK, Q], F32, name=f"q_raw{k}") for k in range(2)]
        for k, src in enumerate((query, dquery)):
            nc.sync.dma_start(q_raw[k][:], src.rearrange("(p t) q -> p t q", t=PACK))
        pool_vals = [sb.tile([P, T], F32, name=f"pool_vals{c}", tag=f"plane{c}", align_bytes=64) for c in range(PLANES)]
        th_sb = sb.tile([P, 1], F32, name="th_sb")
        sharp_sb = sb.tile([P, 1], F32, name="sharp_sb")
        os_sb = sb.tile([P, PACK], F32, name="os_sb")
        nc.sync.dma_start(pool_vals[0][:], vals[0:P, :])
        nc.sync.dma_start(sharp_sb[:], sharp)
        nc.sync.dma_start(th_sb[:], th)
        nc.sync.dma_start(pool_vals[1][:], vals[P : 2 * P, :])
        nc.sync.dma_start(os_sb[:], slot_factor.rearrange("o (p t) -> (o p) t", t=PACK))
        for c in range(2, PLANES):
            nc.sync.dma_start(pool_vals[c][:], vals[c * P : (c + 1) * P, :])

        ident = sb.tile([P, P], F32, name="ident")
        make_identity(nc, ident[:])
        neg_th = sb.tile([P, 1], F32, name="neg_th")
        nc.scalar.activation(neg_th[:], th_sb[:], ACT.Copy, scale=-1.0)
        neg_sharp = sb.tile([P, 1], F32, name="neg_sharp")
        nc.scalar.activation(neg_sharp[:], sharp_sb[:], ACT.Copy, scale=-1.0 / PAGE)

        key_words = sb.tile([P, I], U16, name="key_words", align_bytes=64)
        nc.vector.tensor_copy(key_words[:], words[:].indirect(offsets[:]))
        key_scales = sb.tile([P, I], U8, name="key_scales", align_bytes=64)
        nc.vector.tensor_copy(key_scales[:], kscales[:].indirect(offsets[:]))

        q_bf = sb.tile([P, 2, Q, PACK], BF16, name="q_bf", align_bytes=64)
        for k in range(2):
            nc.scalar.copy(
                q_bf[:, k].rearrange("p (c i) t -> p c t i", i=4),
                q_raw[k][:].rearrange("p t (c i) -> p c t i", i=4),
            )
        q_codes = sb.tile([P, 2 * Q], U32, name="q_codes", align_bytes=64)
        q_scales = sb.tile([P, 2 * Q], U8, name="q_scales", align_bytes=64)
        nc.vector.quantize_mx(
            out=q_codes[:].bitcast(FP8X4), scales=q_scales[:], in_=q_bf[:].rearrange("p k q t -> p (k q t)")
        )
        a_ps = ps.tile([P, I], F32, name="a_ps")
        ta_ps = ps.tile([P, I], F32, name="ta_ps")
        for k, bank in enumerate((a_ps, ta_ps)):
            nc.tensor.matmul_mx(
                out=bank[:],
                lhsT=q_codes[:, k * Q : (k + 1) * Q].bitcast(FP8X4),
                lhsT_scale=q_scales[:, k * Q : (k + 1) * Q],
                rhs=key_words[:].bitcast(FP4X4),
                rhs_scale=key_scales[:],
                start=True,
                stop=True,
            )

        def gather_plane(c):
            picked = sb.tile([P, I], BF16, name=f"picked{c}", tag=f"picked{c}", align_bytes=64)
            nc.vector.tensor_copy(picked[:], pool_vals[c][:].indirect(offsets[:]))
            pairs = picked[:].bitcast(F32)
            turned = ps.tile([P, 2, P], F32, name="turned", tag="turned", bufs=2)
            for u in range(2):
                nc.tensor.transpose(turned[:, u, :], pairs[:, u : I // 2 : 2], ident[:])
            return turned

        def weave_plane(v_bf, turned):
            nc.scalar.copy(
                v_bf.bitcast(F32).rearrange("p (e u) -> p e u", u=2), turned[:].rearrange("p u e -> p e u")
            )

        def quantise(name, values, tag=""):
            width = values.shape[1] // PACK
            codes = sb.tile([P, width], U32, name=f"{name}_codes", tag=tag, align_bytes=64)
            scales = sb.tile([P, width], U8, name=f"{name}_scales", align_bytes=64)
            nc.vector.quantize_mx(out=codes[:].bitcast(FP8X4), scales=scales[:], in_=values)
            return codes, scales

        dealt = "q (p t) -> q t p"
        a_sum = sb.tile([P, G], F32, name="a_sum", tag="picked0", align_bytes=64)
        ta_sum = sb.tile([P, G], F32, name="ta_sum")
        nc.vector.tensor_reduce(a_sum[:], a_ps[:].rearrange("q (g j) -> q g j", j=PAGE), AX.X, ALU.add)
        neg_s = sb.tile([P, G], F32, name="neg_s")
        neg_max = sb.tile([P, 1], F32, name="neg_max", tag="gate", align_bytes=64)
        nc.vector.tensor_scalar(neg_s[:], a_sum[:], neg_sharp[:], None, ALU.mult, ALU.min, accum_out=neg_max[:])
        nc.vector.tensor_reduce(ta_sum[:], ta_ps[:].rearrange("q (g j) -> q g j", j=PAGE), AX.X, ALU.add)
        by_part = [P, G, PARTS_PER_PAGE]
        pexp = sb.tile(by_part, F32, name="pexp")
        z4 = sb.tile([P, 1], F32, name="z4")
        nc.scalar.activation(
            pexp[:], neg_s[:].unsqueeze(2).to_broadcast(by_part), ACT.Exp, bias=neg_max[:], scale=-1.0, accum_out=z4[:]
        )
        turned0 = gather_plane(0)

        gate = sb.tile([P, PACK, P], F32, name="gate", tag="gate", align_bytes=64)
        nc.scalar.activation(gate[:], a_ps[:].rearrange(dealt, t=PACK), ACT.Sigmoid, bias=neg_th[:])
        v_bf0 = sb.tile([P, P * PACK], BF16, name="v_bf0", align_bytes=64)
        weave_plane(v_bf0[:], turned0)
        v_bf12 = sb.tile([P, 2, P * PACK], BF16, name="v_bf12", align_bytes=64)
        weave_plane(v_bf12[:, 0, :], gather_plane(1))
        neg_os4 = sb.tile([P, PACK], F32, name="neg_os4")
        nc.scalar.activation(neg_os4[:], os_sb[:], ACT.Copy, scale=-1.0 * PARTS_PER_PAGE)
        gate_t = ps.tile([P, PACK, Q], F32, name="gate_t")
        for t in range(PACK):
            nc.tensor.transpose(gate_t[:, t, :], gate[:, t, :], ident[:])
        gate_os = sb.tile([P, PACK, Q], F32, name="gate_os", tag="gate_os", align_bytes=64)
        for t in range(PACK):
            nc.scalar.activation(gate_os[:, t, :], gate_t[:, t, :], ACT.Copy, scale=neg_os4[:, t : t + 1])

        inv_z4 = sb.tile([P, 1], F32, name="inv_z4")
        nc.vector.reciprocal(inv_z4[:], z4[:])
        neg_tp = sb.tile(by_part, F32, name="neg_tp")
        neg_tz4 = sb.tile([P, 1], F32, name="neg_tz4")
        nc.vector.scalar_tensor_tensor(
            neg_tp[:], ta_sum[:].unsqueeze(2).to_broadcast(by_part), neg_sharp[:], pexp[:],
            ALU.mult, ALU.mult, accum_out=neg_tz4[:],
        )
        inv_sq = sb.tile([P, 1], F32, name="inv_sq")
        nc.vector.tensor_tensor(inv_sq[:], inv_z4[:], inv_z4[:], ALU.mult)
        tar = sb.tile([P, PACK, P], F32, name="tar", tag="picked2", align_bytes=64)
        nc.vector.scalar_tensor_tensor(
            tar[:], ta_ps[:].rearrange(dealt, t=PACK), inv_z4[:],
            pexp[:].rearrange("q g j -> q (g j)").unsqueeze(1).to_broadcast([P, PACK, P]), ALU.mult, ALU.mult,
        )
        mean_term = sb.tile(by_part, F32, name="mean_term")
        nc.vector.tensor_scalar(mean_term[:], pexp[:], neg_tz4[:], inv_sq[:], ALU.mult, ALU.mult)
        tshare = sb.tile(by_part, F32, name="tshare")
        nc.vector.scalar_tensor_tensor(tshare[:], neg_tp[:], inv_z4[:], mean_term[:], ALU.mult, ALU.subtract)
        xr = sb.tile([P, PACK, P], F32, name="xr", tag="plane1", align_bytes=64)
        nc.vector.scalar_tensor_tensor(xr[:], gate[:], 1.0, tar[:], ALU.subtract, ALU.mult)
        v0_codes, v0_scales = quantise("v0", v_bf0[:])
        inner_t = ps.tile([P, PACK, Q], F32, name="inner_t")
        for t in range(PACK):
            nc.tensor.matmul(inner_t[:, t, :], xr[:, t, :], ident[:], start=True, stop=False, is_transpose=True)
            nc.tensor.matmul(
                inner_t[:, t, :], tshare[:].rearrange("q g j -> q (g j)"), ident[:],
                start=False, stop=True, is_transpose=True,
            )
        weave_plane(v_bf12[:, 1, :], gather_plane(2))
        v_bf3 = sb.tile([P, P * PACK], BF16, name="v_bf3", align_bytes=64)
        weave_plane(v_bf3[:], gather_plane(3))
        w_bf = sb.tile([P, Q, PACK], BF16, name="w_bf", tag="plane3", align_bytes=64)
        nc.vector.tensor_tensor(
            w_bf[:].rearrange("p (c i) t -> p c t i", i=4),
            inner_t[:].rearrange("p t (c i) -> p c t i", i=4),
            gate_os[:].rearrange("p t (c i) -> p c t i", i=4),
            ALU.mult,
        )
        w_codes, w_scales = quantise("w", w_bf[:].rearrange("p q t -> p (q t)"))
        v12_codes, v12_scales = quantise("v12", v_bf12[:].rearrange("p c x -> p (c x)"), tag="gate_os")
        v3_codes, v3_scales = quantise("v3", v_bf3[:])

        def weigh(bank, codes, scales):
            nc.tensor.matmul_mx(
                out=bank,
                lhsT=w_codes[:].bitcast(FP8X4),
                lhsT_scale=w_scales[:],
                rhs=codes[:].bitcast(FP8X4),
                rhs_scale=scales[:],
                start=True,
                stop=True,
            )

        head_ps = ps.tile([P, 3 * P], F32, name="head_ps")
        weigh(head_ps[:, 0:P], v0_codes, v0_scales)
        weigh(head_ps[:, P : 3 * P], v12_codes, v12_scales)
        tail_ps = ps.tile([P, P], F32, name="tail_ps")
        weigh(tail_ps[:], v3_codes, v3_scales)
        head_sb = sb.tile([P, 3 * P], F32, name="head_sb")
        nc.scalar.copy(head_sb[:], head_ps[:])
        nc.sync.dma_start(out[:, 0 : 3 * P], head_sb[:])
        tail_sb = sb.tile([P, P], F32, name="tail_sb")
        nc.vector.tensor_copy(tail_sb[:], tail_ps[:])
        nc.sync.dma_start(out[:, 3 * P : E], tail_sb[:])
